import numpy as np
import ml_dtypes


def mxq(x, axis, fmt="e4m3"):
    dtype, down = {"e4m3": (ml_dtypes.float8_e4m3fn, 7), "e5m2": (ml_dtypes.float8_e5m2, 14)}[fmt]
    v = np.moveaxis(np.asarray(x, np.float32).astype(ml_dtypes.bfloat16).astype(np.float64), axis, -1)
    blocks = v.reshape(v.shape[:-1] + (-1, 32))
    amax = np.abs(blocks).max(-1, keepdims=True)
    byte = np.maximum(np.where(amax > 0, np.frexp(amax)[1] - 1 + 127, 0) - down, 1)
    scale = np.exp2(byte - 127.0)
    codes = (blocks / scale).astype(np.float32).astype(dtype).astype(np.float64)
    return np.moveaxis((codes * scale).reshape(v.shape), -1, axis)


WIDE = False


def mx_kscale(k):
    if not WIDE:
        return np.ones(k)
    levels = np.array([10, -10, 5, -5, 0])
    if k % 512:
        return np.exp2(np.random.permutation(np.resize(levels, k // 32))).repeat(32)
    a = np.empty((k // 512, 16))
    for p in range(k // 512):
        a[p, :8] = np.random.permutation(np.resize(levels, 8))
        for g in range(8):
            far = levels[np.abs(levels - a[p, g]) >= 10]
            a[p, g + 8] = far[np.random.randint(len(far))]
    return np.exp2(a.ravel()).repeat(32)


def f64(x):
    return np.asarray(x).astype(np.float64)


def striped(idx):
    return np.tile(np.asarray(idx).reshape(-1, 16).T, (8, 1)).astype(np.uint16)


def unstriped(offs):
    return offs[:16].T.reshape(-1).astype(np.int64)


E2M1 = np.array([0.0, 0.5, 1.0, 1.5, 2.0, 3.0, 4.0, 6.0, -0.0, -0.5, -1.0, -1.5, -2.0, -3.0, -4.0, -6.0])


def pack_weight(w, fmt):
    k, n = w.shape
    w = f64(np.asarray(w, np.float32).astype(ml_dtypes.bfloat16)).reshape(k // 32, 32, n)
    amax = np.abs(w).max(1)
    if fmt == "e4m3":
        byte = np.frexp(amax)[1] - 1 + 127 - 7
    else:
        mant, ex = np.frexp(amax / 6.0)
        byte = np.where(mant > 0.5, ex, ex - 1) + 127
    byte = np.clip(np.where(amax > 0, byte, 1), 1, 254)
    scaled = (w * np.exp2(127.0 - byte)[:, None, :]).reshape(k, n).astype(np.float32)
    by_word = np.ascontiguousarray(scaled.reshape(k // 512, 128, 4, n).transpose(0, 1, 3, 2))
    if fmt == "e4m3":
        words = by_word.astype(ml_dtypes.float8_e4m3fn).view(np.uint8)
    else:
        c = by_word.astype(ml_dtypes.float4_e2m1fn).view(np.uint8) & 0xF
        words = (c[..., 0::2] | (c[..., 1::2] << 4)).reshape(k // 512, 128, 2 * n)
    return np.ascontiguousarray(words), np.ascontiguousarray(byte.astype(np.uint8).reshape(k // 512, 16, n))


def unpack_weight(words, scales, fmt):
    g, _, n = scales.shape
    words = np.ascontiguousarray(words).reshape(g, 128, n, -1)
    if fmt == "e4m3":
        vals = words.view(ml_dtypes.float8_e4m3fn).astype(np.float64)
    else:
        nib = np.empty((g, 128, n, 4), np.uint8)
        nib[..., 0::2] = words & 0xF
        nib[..., 1::2] = words >> 4
        vals = E2M1[nib]
    vals = vals * np.repeat(np.exp2(scales.astype(np.float64) - 127.0), 8, axis=1)[..., None]
    return vals.transpose(0, 1, 3, 2).reshape(g * 512, n)


def sigmoid(v):
    return 1.0 / (1.0 + np.exp(-v))


D, E, T, I, Q = 512, 512, 1024, 256, 512


def setup_inputs():
    n = np.random.standard_normal
    idx = np.random.permutation(T)[:I]
    fd = mx_kscale(D)
    fq = mx_kscale(Q)
    keysp = pack_weight(n((D, T)) / fd[:, None], "e2m1")
    return {
        "query": (n((D, Q)) * 0.5 / np.sqrt(D) * fd[:, None]).astype(np.float32),
        "query2": (n((D, Q)) * 0.6 / np.sqrt(D) * fd[:, None]).astype(np.float32),
        "keys_words": keysp[0],
        "keys_scales": keysp[1],
        "age": np.tile(np.random.uniform(0.0, 2.0, T), (128, 1)).astype(np.float32),
        "grace": (np.random.uniform(0.7, 1.5, (Q, 1))).astype(np.float32),
        "size": (np.random.uniform(0.5, 2.0, (1, I))).astype(np.float32),
        "qs": (np.random.uniform(2.0, 8.0, (Q, 1)) * fq[:, None]).astype(np.float32),
        "grows": (n((Q, E)) / fq[:, None]).astype(np.float32),
        "old": (n((E, T)) * 2.0).astype(np.float32),
        "fade": (np.random.uniform(0.5, 1.0, (1, T))).astype(np.float32),
        "offs": striped(idx),
    }


def reference(query, query2, keys_words, keys_scales, age, grace, size, qs, grows, old, fade, offs):
    idx = unstriped(offs)
    keysu = unpack_weight(keys_words, keys_scales, "e2m1")
    queryq = mxq(f64(query), 0, "e4m3")
    keysidxg = keysu[:, idx]
    a = queryq.T @ keysidxg
    query2q = mxq(f64(query2), 0, "e4m3")
    b = query2q.T @ keysidxg
    r = np.exp(a - np.max(a, axis=1, keepdims=True))
    gt = sigmoid((b + f64(grace) - f64(age)[:1][:, idx]) * 3.0)
    p = r * gt
    z = np.sum(p, axis=1, keepdims=True)
    w = p * f64(size) / z
    wq = w * f64(qs)
    growsq = mxq(f64(grows), 0, "e4m3")
    wqq = mxq(wq, 0, "e4m3")
    gv = growsq.T @ wqq
    gf = np.zeros((E, T))
    gf[:, idx] = gv
    y = f64(old) * f64(fade) + gf
    return y

@@ -1,0 +1,185 @@
+from contextlib import ExitStack
+
+import concourse.mybir as mybir
+from concourse.masks import make_identity
+
+D, E, T, I, Q = 512, 512, 1024, 256, 512
+FLOPS = 2 * (2 * D * Q * I + Q * E * I)
+BYTES = 4 * (2 * D * Q + Q * E + 2 * E * T + 2 * T + I + 2 * Q) + 128 * 2 * T + 16 * T + 128 * 16 * 2
+
+F32 = mybir.dt.float32
+BF16 = mybir.dt.bfloat16
+I32 = mybir.dt.int32
+U32 = mybir.dt.uint32
+U16 = mybir.dt.uint16
+U8 = mybir.dt.uint8
+FP8X4 = mybir.dt.float8_e4m3fn_x4
+FP4X4 = mybir.dt.float4_e2m1fn_x4
+ACT = mybir.ActivationFunctionType
+ALU = mybir.AluOpType
+AX = mybir.AxisListType
+
+P = 128
+PACK = 4
+HALF = 256
+
+
+def tile_attend_bsoftlives_b_v_kernel(tc, query, query2, keys_words, keys_scales, age, grace, size, qs, grows, old, fade, offs, out):
+    nc = tc.nc
+    with ExitStack() as ctx:
+        sb = ctx.enter_context(tc.tile_pool(name="sb", bufs=1))
+        ps = ctx.enter_context(tc.psum_pool(name="ps", bufs=1))
+
+        offsets = sb.tile([P, I // 16], U16, name="offsets")
+        key_words = sb.tile([P, T], U16, name="key_words")
+        key_bytes = sb.tile([P, T], U8, name="key_bytes")
+        raw = {}
+        for nm in ("query", "query2", "grows"):
+            for h in range(2):
+                raw[nm, h] = sb.tile([P, PACK, HALF], F32, name="raw_%s%d" % (nm, h))
+        fade_col = sb.tile([P, 8], F32, name="fade_col")
+        size_col = sb.tile([P, 2], F32, name="size_col")
+        grace_t = sb.tile([P, PACK], F32, name="grace_t")
+        qs_t = sb.tile([P, PACK], F32, name="qs_t")
+        olds = [sb.tile([P, T], F32, name="old%d" % k) for k in range(4)]
+        windows = [sb.tile([P, T], F32, name="window%d" % k) for k in range(4)]
+        ident = sb.tile([P, P], F32, name="ident")
+
+        def load_half(src, nm, h):
+            nc.sync.dma_start(out=raw[nm, h][:], in_=src.rearrange("(p j) c -> p j c", j=PACK)[:, :, HALF * h : HALF * (h + 1)])
+
+        age_win = sb.tile([P, T], F32, name="age_win")
+        age_g = sb.tile([P, I], F32, name="age_g")
+        age_col = sb.tile([P, 8], F32, name="age_col")
+        nc.gpsimd.memset(key_bytes[:].bitcast(I32), 0)
+        nc.sync.dma_start(offsets[:], offs)
+        nc.sync.dma_start(out=age_col[:].rearrange("p (h j) -> p h j", j=4), in_=age[0:1, :].rearrange("o (h p j) -> p (o h) j", h=2, j=4))
+        nc.sync.dma_start(out=key_words[:].bitcast(I32), in_=keys_words[0].bitcast(I32))
+        for g in range(4):
+            nc.sync.dma_start(out=key_bytes[32 * g : 32 * g + 4, :].bitcast(I32), in_=keys_scales[0, 4 * g : 4 * g + 4, :].bitcast(I32))
+        load_half(query, "query", 0)
+        load_half(query, "query", 1)
+        load_half(query2, "query2", 0)
+        load_half(query2, "query2", 1)
+        nc.sync.dma_start(out=grace_t[:], in_=grace.rearrange("(p r) o -> p (r o)", r=PACK))
+        nc.sync.dma_start(out=fade_col[:].rearrange("p (h j) -> p h j", j=4), in_=fade.rearrange("o (h p j) -> p (o h) j", h=2, j=4))
+        nc.sync.dma_start(out=size_col[:], in_=size.rearrange("o (p j) -> p (o j)", j=2))
+        nc.sync.dma_start(out=qs_t[:], in_=qs.rearrange("(p r) o -> p (r o)", r=PACK))
+        for k in range(4):
+            if k == 2:
+                load_half(grows, "grows", 0)
+                load_half(grows, "grows", 1)
+            nc.sync.dma_start(out=olds[k][:], in_=old[P * k : P * (k + 1), :])
+
+        make_identity(nc, ident[:])
+
+        def spread(bank, col, first, n):
+            for j in range(n):
+                nc.tensor.transpose(bank[:, j, :], col[:, first + j : first + j + 1].to_broadcast([P, P]), ident[:])
+
+        for h in range(2):
+            bank = ps.tile([P, 4, P], F32, name="age_ps%d" % h, tag="B%d" % h)
+            spread(bank, age_col, 4 * h, 4)
+            nc.scalar.activation(age_win[:, 512 * h : 512 * (h + 1)].rearrange("p (n j) -> p n j", j=4), bank[:].rearrange("p j n -> p n j"), ACT.Copy)
+
+        kg_words = sb.tile([P, I], U16, name="kg_words", align_bytes=64)
+        kg_bytes = sb.tile([P, I], U8, name="kg_bytes", align_bytes=64)
+        nc.vector.tensor_copy(kg_words[:], key_words[:].indirect(offsets[:]))
+        nc.vector.tensor_copy(kg_bytes[:], key_bytes[:].indirect(offsets[:]))
+
+        nc.vector.tensor_copy(age_g[:], age_win[:].indirect(offsets[:]))
+
+        codes = {}
+        scales = {}
+        for nm in ("query", "query2", "grows"):
+            codes[nm] = sb.tile([P, 512], U32, name="codes_" + nm, align_bytes=64)
+            scales[nm] = sb.tile([P, 512], U8, name="scales_" + nm, align_bytes=64)
+
+        dealt = {nm: sb.tile([P, PACK, P, PACK], BF16, name="dealt_" + nm, align_bytes=64) for nm in ("query", "query2")}
+
+        def round_query(nm, h, copy):
+            copy(dealt[nm][:, :, 64 * h : 64 * (h + 1), :].rearrange("p r s j -> p s j r"), raw[nm, h][:].rearrange("p j (s r) -> p s j r", r=PACK))
+
+        def quantise_query(nm):
+            nc.vector.quantize_mx(out=codes[nm][:].bitcast(FP8X4), scales=scales[nm][:], in_=dealt[nm][:].rearrange("p r s j -> p (r s j)"))
+
+        def scores(nm, tag):
+            banks = [ps.tile([P, 2, I], F32, name="%s_ps%d" % (nm, b), tag="%s%d" % (tag, b)) for b in range(2)]
+            for r in range(PACK):
+                cols = slice(P * r, P * (r + 1))
+                nc.tensor.matmul_mx(out=banks[r // 2][:, r % 2, :], lhsT=codes[nm][:, cols].bitcast(FP8X4), lhsT_scale=scales[nm][:, cols],
+                                    rhs=kg_words[:].bitcast(FP4X4), rhs_scale=kg_bytes[:], start=True, stop=True)
+            return banks
+
+        round_query("query", 0, nc.scalar.copy)
+        round_query("query", 1, nc.vector.tensor_copy)
+        quantise_query("query")
+        a_ps = scores("query", "A")
+
+        round_query("query2", 0, nc.vector.tensor_copy)
+        neg_max = sb.tile([P, PACK], F32, name="neg_max")
+        expo = sb.tile([P, PACK, I], F32, name="expo")
+        for b in range(2):
+            nc.vector.tensor_reduce(out=neg_max[:, 2 * b : 2 * b + 2], in_=a_ps[b][:], axis=AX.X, op=ALU.max, negate=True)
+        for r in range(PACK):
+            nc.scalar.activation(expo[:, r, :], a_ps[r // 2][:, r % 2, :], ACT.Exp, bias=neg_max[:, r : r + 1])
+        round_query("query2", 1, nc.vector.tensor_copy)
+        quantise_query("query2")
+        b_ps = scores("query2", "B")
+
+        size_ps = ps.tile([P, 2, P], F32, name="size_ps", tag="F")
+        spread(size_ps, size_col, 0, 2)
+
+        arg = sb.tile([P, PACK, I], F32, name="arg", tag="arg", align_bytes=64)
+        life = sb.tile([P, PACK, I], F32, name="life")
+        for r in range(PACK):
+            nc.vector.scalar_tensor_tensor(out=arg[:, r, :], in0=b_ps[r // 2][:, r % 2, :], scalar=grace_t[:, r : r + 1], in1=age_g[:], op0=ALU.add, op1=ALU.subtract)
+        for r in range(PACK):
+            nc.scalar.activation(life[:, r, :], arg[:, r, :], ACT.Sigmoid, scale=3.0)
+
+        prob = sb.tile([P, PACK, I], F32, name="prob")
+        wq_rows = sb.tile([P, PACK, I], BF16, name="wq_rows")
+        factors = []
+        for b in range(2):
+            total = sb.tile([P, 2], F32, name="total%d" % b)
+            inv = sb.tile([P, 2], F32, name="inv%d" % b)
+            factor = sb.tile([P, 2], F32, name="factor%d" % b)
+            for r in range(2 * b, 2 * b + 2):
+                nc.vector.scalar_tensor_tensor(out=prob[:, r, :], in0=expo[:, r, :], scalar=1.0, in1=life[:, r, :], op0=ALU.mult, op1=ALU.mult, accum_out=total[:, r % 2 : r % 2 + 1])
+            nc.vector.reciprocal(inv[:], total[:])
+            nc.vector.tensor_tensor(factor[:], inv[:], qs_t[:, 2 * b : 2 * b + 2], ALU.mult)
+            factors.append(factor)
+        for r in range(PACK):
+            nc.vector.scalar_tensor_tensor(out=wq_rows[:, r, :].rearrange("p (n j) -> p n j", j=2), in0=prob[:, r, :].rearrange("p (n j) -> p n j", j=2),
+                                           scalar=factors[r // 2][:, r % 2 : r % 2 + 1], in1=size_ps[:].rearrange("p j n -> p n j"), op0=ALU.mult, op1=ALU.mult)
+        fade_ps = ps.tile([P, 8, P], F32, name="fade_ps", tag="F")
+        spread(fade_ps, fade_col, 0, 8)
+        wq_packed = sb.tile([P, I, PACK], BF16, name="wq_packed", align_bytes=64)
+        nc.vector.tensor_copy(wq_packed[:].rearrange("p (c i) r -> p c r i", i=4), wq_rows[:].rearrange("p r (c i) -> p c r i", i=4))
+        wq_codes = sb.tile([P, I], U32, name="wq_codes", align_bytes=64)
+        wq_scales = sb.tile([P, I], U8, name="wq_scales", align_bytes=64)
+        nc.vector.quantize_mx(out=wq_codes[:].bitcast(FP8X4), scales=wq_scales[:], in_=wq_packed[:].rearrange("p i r -> p (i r)"))
+
+        grows_packed = sb.tile([P, 2, HALF, PACK], BF16, name="grows_packed", tag="arg", align_bytes=64)
+        for h in range(2):
+            packed = grows_packed[:, h, :, :]
+            nc.scalar.copy(packed.rearrange("p (c i) j -> p c j i", i=4), raw["grows", h][:].rearrange("p j (c i) -> p c j i", i=4))
+            cols = slice(HALF * h, HALF * (h + 1))
+            nc.vector.quantize_mx(out=codes["grows"][:, cols].bitcast(FP8X4), scales=scales["grows"][:, cols], in_=packed.rearrange("p c j -> p (c j)"))
+
+        for k in range(4):
+            nc.vector.memset(windows[k][:], 0.0)
+        for k in range(4):
+            cols = slice(P * k, P * (k + 1))
+            gv_ps = ps.tile([P, I], F32, name="gv_ps%d" % k, tag=("A0", "A1", "B0", "B1")[k])
+            nc.tensor.matmul_mx(out=gv_ps[:], lhsT=codes["grows"][:, cols].bitcast(FP8X4), lhsT_scale=scales["grows"][:, cols],
+                                rhs=wq_codes[:].bitcast(FP8X4), rhs_scale=wq_scales[:], start=True, stop=True)
+            gv = sb.tile([P, I], F32, name="gv%d" % k)
+            nc.scalar.copy(gv[:], gv_ps[:])
+            nc.scalar.activation(windows[k][:].indirect(offsets[:]), gv[:], ACT.Copy)
+            for h in range(2):
+                part = olds[k][:, 512 * h : 512 * (h + 1)].rearrange("p (n j) -> p n j", j=4)
+                nc.vector.tensor_tensor(part, part, fade_ps[:, 4 * h : 4 * h + 4, :].rearrange("p j n -> p n j"), ALU.mult)
+            for t0, t1 in ([(0, T)] if k < 3 else [(0, 512), (512, 768), (768, T)]):
+                nc.vector.tensor_tensor(olds[k][:, t0:t1], olds[k][:, t0:t1], windows[k][:, t0:t1], ALU.add)
+                nc.sync.dma_start(out=out[P * k : P * (k + 1), t0:t1], in_=olds[k][:, t0:t1])

@@ -41,7 +41,7 @@ def tile_attend_bsoftlives_b_v_kernel(tc, query, query2, keys_words, keys_scales
         size_col = sb.tile([P, 2], F32, name="size_col")
         grace_t = sb.tile([P, PACK], F32, name="grace_t")
         qs_t = sb.tile([P, PACK], F32, name="qs_t")
-        olds = [sb.tile([P, T], F32, name="old%d" % k) for k in range(4)]
+        olds = [sb.tile([P, T], F32, name="old%d" % k, tag="old%d" % k) for k in range(4)]
         windows = [sb.tile([P, T], F32, name="window%d" % k) for k in range(4)]
         ident = sb.tile([P, P], F32, name="ident")
 
@@ -54,33 +54,36 @@ def tile_attend_bsoftlives_b_v_kernel(tc, query, query2, keys_words, keys_scales
         nc.gpsimd.memset(key_bytes[:].bitcast(I32), 0)
         nc.sync.dma_start(offsets[:], offs)
         nc.sync.dma_start(out=age_col[:].rearrange("p (h j) -> p h j", j=4), in_=age[0:1, :].rearrange("o (h p j) -> p (o h) j", h=2, j=4))
+        nc.sync.dma_start(out=fade_col[:].rearrange("p (h j) -> p h j", j=4), in_=fade.rearrange("o (h p j) -> p (o h) j", h=2, j=4))
         nc.sync.dma_start(out=key_words[:].bitcast(I32), in_=keys_words[0].bitcast(I32))
+        load_half(query, "query", 0)
         for g in range(4):
             nc.sync.dma_start(out=key_bytes[32 * g : 32 * g + 4, :].bitcast(I32), in_=keys_scales[0, 4 * g : 4 * g + 4, :].bitcast(I32))
-        load_half(query, "query", 0)
         load_half(query, "query", 1)
         load_half(query2, "query2", 0)
         load_half(query2, "query2", 1)
         nc.sync.dma_start(out=grace_t[:], in_=grace.rearrange("(p r) o -> p (r o)", r=PACK))
-        nc.sync.dma_start(out=fade_col[:].rearrange("p (h j) -> p h j", j=4), in_=fade.rearrange("o (h p j) -> p (o h) j", h=2, j=4))
         nc.sync.dma_start(out=size_col[:], in_=size.rearrange("o (p j) -> p (o j)", j=2))
         nc.sync.dma_start(out=qs_t[:], in_=qs.rearrange("(p r) o -> p (r o)", r=PACK))
+        load_half(grows, "grows", 0)
+        load_half(grows, "grows", 1)
         for k in range(4):
-            if k == 2:
-                load_half(grows, "grows", 0)
-                load_half(grows, "grows", 1)
             nc.sync.dma_start(out=olds[k][:], in_=old[P * k : P * (k + 1), :])
 
         make_identity(nc, ident[:])
 
         def spread(bank, col, first, n):
             for j in range(n):
-                nc.tensor.transpose(bank[:, j, :], col[:, first + j : first + j + 1].to_broadcast([P, P]), ident[:])
+                nc.tensor.transpose(bank.rearrange("p (n j) -> p j n", j=n)[:, j, :], col[:, first + j : first + j + 1].to_broadcast([P, P]), ident[:])
 
         for h in range(2):
-            bank = ps.tile([P, 4, P], F32, name="age_ps%d" % h, tag="B%d" % h)
-            spread(bank, age_col, 4 * h, 4)
-            nc.scalar.activation(age_win[:, 512 * h : 512 * (h + 1)].rearrange("p (n j) -> p n j", j=4), bank[:].rearrange("p j n -> p n j"), ACT.Copy)
+            bank = ps.tile([P, 512], F32, name="age_ps%d" % h, tag="B%d" % h)
+            spread(bank[:], age_col, 4 * h, 4)
+            nc.scalar.activation(age_win[:, 512 * h : 512 * (h + 1)], bank[:], ACT.Copy)
+
+        fade_ps = ps.tile([P, T], F32, name="fade_ps")
+        for h in range(2):
+            spread(fade_ps[:, 512 * h : 512 * (h + 1)], fade_col, 4 * h, 4)
 
         kg_words = sb.tile([P, I], U16, name="kg_words", align_bytes=64)
         kg_bytes = sb.tile([P, I], U8, name="kg_bytes", align_bytes=64)
@@ -97,11 +100,15 @@ def tile_attend_bsoftlives_b_v_kernel(tc, query, query2, keys_words, keys_scales
 
         dealt = {nm: sb.tile([P, PACK, P, PACK], BF16, name="dealt_" + nm, align_bytes=64) for nm in ("query", "query2")}
 
-        def round_query(nm, h, copy):
-            copy(dealt[nm][:, :, 64 * h : 64 * (h + 1), :].rearrange("p r s j -> p s j r"), raw[nm, h][:].rearrange("p j (s r) -> p s j r", r=PACK))
+        def round_query(nm, s0, s1, copy):
+            h = s0 // 64
+            src = raw[nm, h][:, :, PACK * (s0 - 64 * h) : PACK * (s1 - 64 * h)]
+            copy(dealt[nm][:, :, s0:s1, :].rearrange("p r s j -> p s j r"), src.rearrange("p j (s r) -> p s j r", r=PACK))
 
         def quantise_query(nm):
-            nc.vector.quantize_mx(out=codes[nm][:].bitcast(FP8X4), scales=scales[nm][:], in_=dealt[nm][:].rearrange("p r s j -> p (r s j)"))
+            for b in range(2):
+                cols = slice(HALF * b, HALF * (b + 1))
+                nc.vector.quantize_mx(out=codes[nm][:, cols].bitcast(FP8X4), scales=scales[nm][:, cols], in_=dealt[nm][:, 2 * b : 2 * b + 2, :, :].rearrange("p r s j -> p (r s j)"))
 
         def scores(nm, tag):
             banks = [ps.tile([P, 2, I], F32, name="%s_ps%d" % (nm, b), tag="%s%d" % (tag, b)) for b in range(2)]
@@ -111,25 +118,25 @@ def tile_attend_bsoftlives_b_v_kernel(tc, query, query2, keys_words, keys_scales
                                     rhs=kg_words[:].bitcast(FP4X4), rhs_scale=kg_bytes[:], start=True, stop=True)
             return banks
 
-        round_query("query", 0, nc.scalar.copy)
-        round_query("query", 1, nc.vector.tensor_copy)
+        round_query("query", 0, 64, nc.scalar.copy)
+        round_query("query", 64, 128, nc.vector.tensor_copy)
         quantise_query("query")
         a_ps = scores("query", "A")
 
-        round_query("query2", 0, nc.vector.tensor_copy)
+        round_query("query2", 0, 64, nc.scalar.copy)
         neg_max = sb.tile([P, PACK], F32, name="neg_max")
         expo = sb.tile([P, PACK, I], F32, name="expo")
         for b in range(2):
             nc.vector.tensor_reduce(out=neg_max[:, 2 * b : 2 * b + 2], in_=a_ps[b][:], axis=AX.X, op=ALU.max, negate=True)
         for r in range(PACK):
             nc.scalar.activation(expo[:, r, :], a_ps[r // 2][:, r % 2, :], ACT.Exp, bias=neg_max[:, r : r + 1])
-        round_query("query2", 1, nc.vector.tensor_copy)
+        round_query("query2", 64, 128, nc.vector.tensor_copy)
         quantise_query("query2")
         b_ps = scores("query2", "B")
 
-        size_ps = ps.tile([P, 2, P], F32, name="size_ps", tag="F")
-        spread(size_ps, size_col, 0, 2)
 
+        size_ps = ps.tile([P, I], F32, name="size_ps")
+        spread(size_ps[:], size_col, 0, 2)
         arg = sb.tile([P, PACK, I], F32, name="arg", tag="arg", align_bytes=64)
         life = sb.tile([P, PACK, I], F32, name="life")
         for r in range(PACK):
@@ -150,11 +157,8 @@ def tile_attend_bsoftlives_b_v_kernel(tc, query, query2, keys_words, keys_scales
             nc.vector.tensor_tensor(factor[:], inv[:], qs_t[:, 2 * b : 2 * b + 2], ALU.mult)
             factors.append(factor)
         for r in range(PACK):
-            nc.vector.scalar_tensor_tensor(out=wq_rows[:, r, :].rearrange("p (n j) -> p n j", j=2), in0=prob[:, r, :].rearrange("p (n j) -> p n j", j=2),
-                                           scalar=factors[r // 2][:, r % 2 : r % 2 + 1], in1=size_ps[:].rearrange("p j n -> p n j"), op0=ALU.mult, op1=ALU.mult)
-        fade_ps = ps.tile([P, 8, P], F32, name="fade_ps", tag="F")
-        spread(fade_ps, fade_col, 0, 8)
-        wq_packed = sb.tile([P, I, PACK], BF16, name="wq_packed", align_bytes=64)
+            nc.vector.scalar_tensor_tensor(out=wq_rows[:, r, :], in0=prob[:, r, :], scalar=factors[r // 2][:, r % 2 : r % 2 + 1], in1=size_ps[:], op0=ALU.mult, op1=ALU.mult)
+        wq_packed = sb.tile([P, I, PACK], BF16, name="wq_packed", tag="wq_packed", align_bytes=64)
         nc.vector.tensor_copy(wq_packed[:].rearrange("p (c i) r -> p c r i", i=4), wq_rows[:].rearrange("p r (c i) -> p c r i", i=4))
         wq_codes = sb.tile([P, I], U32, name="wq_codes", align_bytes=64)
         wq_scales = sb.tile([P, I], U8, name="wq_scales", align_bytes=64)
@@ -169,17 +173,50 @@ def tile_attend_bsoftlives_b_v_kernel(tc, query, query2, keys_words, keys_scales
 
         for k in range(4):
             nc.vector.memset(windows[k][:], 0.0)
+        gv_first = ps.tile([P, I], F32, name="gv_first", tag="A0")
+        gv_pair = ps.tile([P, 2, I], F32, name="gv_pair", tag="A1")
+        gv_last = ps.tile([P, I], F32, name="gv_last", tag="B0")
+        gv_banks = [gv_first[:], gv_pair[:, 0, :], gv_pair[:, 1, :], gv_last[:]]
         for k in range(4):
             cols = slice(P * k, P * (k + 1))
-            gv_ps = ps.tile([P, I], F32, name="gv_ps%d" % k, tag=("A0", "A1", "B0", "B1")[k])
-            nc.tensor.matmul_mx(out=gv_ps[:], lhsT=codes["grows"][:, cols].bitcast(FP8X4), lhsT_scale=scales["grows"][:, cols],
+            nc.tensor.matmul_mx(out=gv_banks[k], lhsT=codes["grows"][:, cols].bitcast(FP8X4), lhsT_scale=scales["grows"][:, cols],
                                 rhs=wq_codes[:].bitcast(FP8X4), rhs_scale=wq_scales[:], start=True, stop=True)
-            gv = sb.tile([P, I], F32, name="gv%d" % k)
-            nc.scalar.copy(gv[:], gv_ps[:])
-            nc.scalar.activation(windows[k][:].indirect(offsets[:]), gv[:], ACT.Copy)
-            for h in range(2):
-                part = olds[k][:, 512 * h : 512 * (h + 1)].rearrange("p (n j) -> p n j", j=4)
-                nc.vector.tensor_tensor(part, part, fade_ps[:, 4 * h : 4 * h + 4, :].rearrange("p j n -> p n j"), ALU.mult)
-            for t0, t1 in ([(0, T)] if k < 3 else [(0, 512), (512, 768), (768, T)]):
-                nc.vector.tensor_tensor(olds[k][:, t0:t1], olds[k][:, t0:t1], windows[k][:, t0:t1], ALU.add)
-                nc.sync.dma_start(out=out[P * k : P * (k + 1), t0:t1], in_=olds[k][:, t0:t1])
+        gv0 = sb.tile([P, I], F32, name="gv0")
+        gv12 = sb.tile([P, 2, I], F32, name="gv12")
+        gv3 = sb.tile([P, I], F32, name="gv3")
+        gvs = [gv0[:], gv12[:, 0, :], gv12[:, 1, :], gv3[:]]
+
+        faded = [sb.tile([P, T], F32, name="faded0", tag="wq_packed", align_bytes=64), sb.tile([P, T], F32, name="faded1", tag="arg", align_bytes=64),
+                 sb.tile([P, T], F32, name="faded2", tag="old0"), sb.tile([P, T], F32, name="faded3", tag="old1")]
+
+        def fade_half(k, h):
+            cols = slice(512 * h, 512 * (h + 1))
+            nc.vector.tensor_tensor(faded[k][:, cols], olds[k][:, cols], fade_ps[:, cols], ALU.mult)
+
+        def finish(k, t0, t1, engine):
+            acc = faded[k][:, t0:t1]
+            engine.tensor_tensor(acc, acc, windows[k][:, t0:t1], ALU.add)
+            nc.sync.dma_start(out=out[P * k : P * (k + 1), t0:t1], in_=acc)
+
+        def scatter(k):
+            nc.scalar.activation(windows[k][:].indirect(offsets[:]), gvs[k], ACT.Copy)
+
+        nc.scalar.copy(gv0[:], gv_first[:])
+        scatter(0)
+        nc.scalar.copy(gv12[:], gv_pair[:])
+        nc.scalar.copy(gv3[:], gv_last[:])
+        for k in range(1, 4):
+            scatter(k)
+
+        for k in range(2):
+            fade_half(k, 0)
+            fade_half(k, 1)
+        finish(0, 0, T, nc.vector)
+        fade_half(2, 0)
+        fade_half(2, 1)
+        finish(1, 0, T, nc.vector)
+        fade_half(3, 0)
+        finish(2, 0, T, nc.vector)
+        fade_half(3, 1)
+        for t0, t1 in ((0, 512), (512, 768), (768, T)):
+            finish(3, t0, t1, nc.vector)

@@ -36,8 +36,8 @@ def tile_attend_bsoftlives_b_v_kernel(tc, query, query2, keys_words, keys_scales
         raw = {}
         for nm in ("query", "query2", "grows"):
             for h in range(2):
-                raw[nm, h] = sb.tile([P, PACK, HALF], F32, name="raw_%s%d" % (nm, h))
-        fade_col = sb.tile([P, 8], F32, name="fade_col")
+                raw[nm, h] = sb.tile([P, PACK, HALF], F32, name="raw_%s%d" % (nm, h), tag="raw_%s%d" % (nm, h))
+        fade_col = sb.tile([P, 2, 8], F32, name="fade_col")
         size_col = sb.tile([P, 2], F32, name="size_col")
         grace_t = sb.tile([P, PACK], F32, name="grace_t")
         qs_t = sb.tile([P, PACK], F32, name="qs_t")
@@ -48,13 +48,11 @@ def tile_attend_bsoftlives_b_v_kernel(tc, query, query2, keys_words, keys_scales
         def load_half(src, nm, h):
             nc.sync.dma_start(out=raw[nm, h][:], in_=src.rearrange("(p j) c -> p j c", j=PACK)[:, :, HALF * h : HALF * (h + 1)])
 
-        age_win = sb.tile([P, T], F32, name="age_win")
+        age_col = sb.tile([P, 2, 8], F32, name="age_col")
         age_g = sb.tile([P, I], F32, name="age_g")
-        age_col = sb.tile([P, 8], F32, name="age_col")
         nc.gpsimd.memset(key_bytes[:].bitcast(I32), 0)
         nc.sync.dma_start(offsets[:], offs)
-        nc.sync.dma_start(out=age_col[:].rearrange("p (h j) -> p h j", j=4), in_=age[0:1, :].rearrange("o (h p j) -> p (o h) j", h=2, j=4))
-        nc.sync.dma_start(out=fade_col[:].rearrange("p (h j) -> p h j", j=4), in_=fade.rearrange("o (h p j) -> p (o h) j", h=2, j=4))
+        nc.sync.dma_start(out=age_col[:, :, 0:4], in_=age[0:1, :].rearrange("o (h p j) -> p (o h) j", h=2, j=4))
         nc.sync.dma_start(out=key_words[:].bitcast(I32), in_=keys_words[0].bitcast(I32))
         load_half(query, "query", 0)
         for g in range(4):
@@ -65,6 +63,7 @@ def tile_attend_bsoftlives_b_v_kernel(tc, query, query2, keys_words, keys_scales
         nc.sync.dma_start(out=grace_t[:], in_=grace.rearrange("(p r) o -> p (r o)", r=PACK))
         nc.sync.dma_start(out=size_col[:], in_=size.rearrange("o (p j) -> p (o j)", j=2))
         nc.sync.dma_start(out=qs_t[:], in_=qs.rearrange("(p r) o -> p (r o)", r=PACK))
+        nc.sync.dma_start(out=fade_col[:, :, 0:4], in_=fade.rearrange("o (h p j) -> p (o h) j", h=2, j=4))
         load_half(grows, "grows", 0)
         load_half(grows, "grows", 1)
         for k in range(4):
@@ -76,21 +75,10 @@ def tile_attend_bsoftlives_b_v_kernel(tc, query, query2, keys_words, keys_scales
             for j in range(n):
                 nc.tensor.transpose(bank.rearrange("p (n j) -> p j n", j=n)[:, j, :], col[:, first + j : first + j + 1].to_broadcast([P, P]), ident[:])
 
-        for h in range(2):
-            bank = ps.tile([P, 512], F32, name="age_ps%d" % h, tag="B%d" % h)
-            spread(bank[:], age_col, 4 * h, 4)
-            nc.scalar.activation(age_win[:, 512 * h : 512 * (h + 1)], bank[:], ACT.Copy)
-
-        fade_ps = ps.tile([P, T], F32, name="fade_ps")
-        for h in range(2):
-            spread(fade_ps[:, 512 * h : 512 * (h + 1)], fade_col, 4 * h, 4)
-
         kg_words = sb.tile([P, I], U16, name="kg_words", align_bytes=64)
         kg_bytes = sb.tile([P, I], U8, name="kg_bytes", align_bytes=64)
         nc.vector.tensor_copy(kg_words[:], key_words[:].indirect(offsets[:]))
         nc.vector.tensor_copy(kg_bytes[:], key_bytes[:].indirect(offsets[:]))
-
-        nc.vector.tensor_copy(age_g[:], age_win[:].indirect(offsets[:]))
 
         codes = {}
         scales = {}
@@ -119,6 +107,11 @@ def tile_attend_bsoftlives_b_v_kernel(tc, query, query2, keys_words, keys_scales
             return banks
 
         round_query("query", 0, 64, nc.scalar.copy)
+        age_win = sb.tile([P, T], F32, name="age_win", tag="raw_query0")
+        for h in range(2):
+            bank = ps.tile([P, 512], F32, name="age_ps%d" % h, tag="B%d" % h)
+            spread(bank[:], age_col[:, h, :], 0, 4)
+            nc.scalar.activation(age_win[:, 512 * h : 512 * (h + 1)], bank[:], ACT.Copy)
         round_query("query", 64, 128, nc.vector.tensor_copy)
         quantise_query("query")
         a_ps = scores("query", "A")
@@ -130,6 +123,7 @@ def tile_attend_bsoftlives_b_v_kernel(tc, query, query2, keys_words, keys_scales
             nc.vector.tensor_reduce(out=neg_max[:, 2 * b : 2 * b + 2], in_=a_ps[b][:], axis=AX.X, op=ALU.max, negate=True)
         for r in range(PACK):
             nc.scalar.activation(expo[:, r, :], a_ps[r // 2][:, r % 2, :], ACT.Exp, bias=neg_max[:, r : r + 1])
+        nc.vector.tensor_copy(age_g[:], age_win[:].indirect(offsets[:]))
         round_query("query2", 64, 128, nc.vector.tensor_copy)
         quantise_query("query2")
         b_ps = scores("query2", "B")
@@ -143,6 +137,10 @@ def tile_attend_bsoftlives_b_v_kernel(tc, query, query2, keys_words, keys_scales
             nc.vector.scalar_tensor_tensor(out=arg[:, r, :], in0=b_ps[r // 2][:, r % 2, :], scalar=grace_t[:, r : r + 1], in1=age_g[:], op0=ALU.add, op1=ALU.subtract)
         for r in range(PACK):
             nc.scalar.activation(life[:, r, :], arg[:, r, :], ACT.Sigmoid, scale=3.0)
+
+        fade_ps = [ps.tile([P, 512], F32, name="fade_ps%d" % h, tag="B%d" % h) for h in range(2)]
+        for h in range(2):
+            spread(fade_ps[h][:], fade_col[:, h, :], 0, 4)
 
         prob = sb.tile([P, PACK, I], F32, name="prob")
         wq_rows = sb.tile([P, PACK, I], BF16, name="wq_rows")
@@ -175,7 +173,7 @@ def tile_attend_bsoftlives_b_v_kernel(tc, query, query2, keys_words, keys_scales
             nc.vector.memset(windows[k][:], 0.0)
         gv_first = ps.tile([P, I], F32, name="gv_first", tag="A0")
         gv_pair = ps.tile([P, 2, I], F32, name="gv_pair", tag="A1")
-        gv_last = ps.tile([P, I], F32, name="gv_last", tag="B0")
+        gv_last = ps.tile([P, I], F32, name="gv_last")
         gv_banks = [gv_first[:], gv_pair[:, 0, :], gv_pair[:, 1, :], gv_last[:]]
         for k in range(4):
             cols = slice(P * k, P * (k + 1))
@@ -191,7 +189,7 @@ def tile_attend_bsoftlives_b_v_kernel(tc, query, query2, keys_words, keys_scales
 
         def fade_half(k, h):
             cols = slice(512 * h, 512 * (h + 1))
-            nc.vector.tensor_tensor(faded[k][:, cols], olds[k][:, cols], fade_ps[:, cols], ALU.mult)
+            nc.vector.tensor_tensor(faded[k][:, cols], olds[k][:, cols], fade_ps[h][:], ALU.mult)
 
         def finish(k, t0, t1, engine):
             acc = faded[k][:, t0:t1]
@@ -202,20 +200,18 @@ def tile_attend_bsoftlives_b_v_kernel(tc, query, query2, keys_words, keys_scales
             nc.scalar.activation(windows[k][:].indirect(offsets[:]), gvs[k], ACT.Copy)
 
         nc.scalar.copy(gv0[:], gv_first[:])
-        scatter(0)
-        nc.scalar.copy(gv12[:], gv_pair[:])
-        nc.scalar.copy(gv3[:], gv_last[:])
-        for k in range(1, 4):
+        fade_half(0, 0)
+        fade_half(0, 1)
+        nc.vector.tensor_copy(gv12[:], gv_pair[:])
+        nc.vector.tensor_copy(gv3[:], gv_last[:])
+        for k in range(4):
             scatter(k)
-
-        for k in range(2):
+        finish(0, 0, T, nc.gpsimd)
+        for k in (1, 2):
             fade_half(k, 0)
             fade_half(k, 1)
-        finish(0, 0, T, nc.vector)
-        fade_half(2, 0)
-        fade_half(2, 1)
-        finish(1, 0, T, nc.vector)
         fade_half(3, 0)
+        finish(1, 0, T, nc.vector)
         finish(2, 0, T, nc.vector)
         fade_half(3, 1)
         for t0, t1 in ((0, 512), (512, 768), (768, T)):

@@ -91,7 +91,8 @@ def tile_attend_bsoftlives_b_v_kernel(tc, query, query2, keys_words, keys_scales
         def round_query(nm, s0, s1, copy):
             h = s0 // 64
             src = raw[nm, h][:, :, PACK * (s0 - 64 * h) : PACK * (s1 - 64 * h)]
-            copy(dealt[nm][:, :, s0:s1, :].rearrange("p r s j -> p s j r"), src.rearrange("p j (s r) -> p s j r", r=PACK))
+            for b in range(2):
+                copy(dealt[nm][:, 2 * b : 2 * b + 2, s0:s1, :].rearrange("p r s j -> p s j r"), src.rearrange("p j (s r) -> p s j r", r=PACK)[:, :, :, 2 * b : 2 * b + 2])
 
         def quantise_query(nm):
             for b in range(2):
@@ -157,10 +158,14 @@ def tile_attend_bsoftlives_b_v_kernel(tc, query, query2, keys_words, keys_scales
         for r in range(PACK):
             nc.vector.scalar_tensor_tensor(out=wq_rows[:, r, :], in0=prob[:, r, :], scalar=factors[r // 2][:, r % 2 : r % 2 + 1], in1=size_ps[:], op0=ALU.mult, op1=ALU.mult)
         wq_packed = sb.tile([P, I, PACK], BF16, name="wq_packed", tag="wq_packed", align_bytes=64)
-        nc.vector.tensor_copy(wq_packed[:].rearrange("p (c i) r -> p c r i", i=4), wq_rows[:].rearrange("p r (c i) -> p c r i", i=4))
         wq_codes = sb.tile([P, I], U32, name="wq_codes", align_bytes=64)
         wq_scales = sb.tile([P, I], U8, name="wq_scales", align_bytes=64)
-        nc.vector.quantize_mx(out=wq_codes[:].bitcast(FP8X4), scales=wq_scales[:], in_=wq_packed[:].rearrange("p i r -> p (i r)"))
+        for h in range(2):
+            cols = slice(P * h, P * (h + 1))
+            nc.vector.tensor_copy(wq_packed[:, cols, :].rearrange("p (c i) r -> p c r i", i=4), wq_rows[:, :, cols].rearrange("p r (c i) -> p c r i", i=4))
+        for h in range(2):
+            cols = slice(P * h, P * (h + 1))
+            nc.vector.quantize_mx(out=wq_codes[:, cols].bitcast(FP8X4), scales=wq_scales[:, cols], in_=wq_packed[:, cols, :].rearrange("p i r -> p (i r)"))
 
         grows_packed = sb.tile([P, 2, HALF, PACK], BF16, name="grows_packed", tag="arg", align_bytes=64)
         for h in range(2):
@@ -171,18 +176,20 @@ def tile_attend_bsoftlives_b_v_kernel(tc, query, query2, keys_words, keys_scales
 
         for k in range(4):
             nc.vector.memset(windows[k][:], 0.0)
-        gv_first = ps.tile([P, I], F32, name="gv_first", tag="A0")
-        gv_pair = ps.tile([P, 2, I], F32, name="gv_pair", tag="A1")
-        gv_last = ps.tile([P, I], F32, name="gv_last")
-        gv_banks = [gv_first[:], gv_pair[:, 0, :], gv_pair[:, 1, :], gv_last[:]]
-        for k in range(4):
+        fade_sb = sb.tile([P, T], F32, name="fade_sb")
+        for h in range(2):
+            nc.scalar.copy(fade_sb[:, 512 * h : 512 * (h + 1)], fade_ps[h][:])
+
+        gv_head = ps.tile([P, P], F32, name="gv_head", tag="A0")
+        gv_mid = ps.tile([P, P + I], F32, name="gv_mid", tag="A1")
+        gv_tail = ps.tile([P, 2 * I], F32, name="gv_tail")
+        for dst, k, i0, i1 in ((gv_head[:], 0, 0, P), (gv_mid[:, 0:P], 0, P, I), (gv_mid[:, P : P + I], 1, 0, I), (gv_tail[:, 0:I], 2, 0, I), (gv_tail[:, I : 2 * I], 3, 0, I)):
             cols = slice(P * k, P * (k + 1))
-            nc.tensor.matmul_mx(out=gv_banks[k], lhsT=codes["grows"][:, cols].bitcast(FP8X4), lhsT_scale=scales["grows"][:, cols],
-                                rhs=wq_codes[:].bitcast(FP8X4), rhs_scale=wq_scales[:], start=True, stop=True)
-        gv0 = sb.tile([P, I], F32, name="gv0")
-        gv12 = sb.tile([P, 2, I], F32, name="gv12")
-        gv3 = sb.tile([P, I], F32, name="gv3")
-        gvs = [gv0[:], gv12[:, 0, :], gv12[:, 1, :], gv3[:]]
+            nc.tensor.matmul_mx(out=dst, lhsT=codes["grows"][:, cols].bitcast(FP8X4), lhsT_scale=scales["grows"][:, cols],
+                                rhs=wq_codes[:, i0:i1].bitcast(FP8X4), rhs_scale=wq_scales[:, i0:i1], start=True, stop=True)
+        head = sb.tile([P, P], F32, name="head")
+        mid = sb.tile([P, P + I], F32, name="mid")
+        tail = sb.tile([P, 2 * I], F32, name="tail")
 
         faded = [sb.tile([P, T], F32, name="faded0", tag="wq_packed", align_bytes=64), sb.tile([P, T], F32, name="faded1", tag="arg", align_bytes=64),
                  sb.tile([P, T], F32, name="faded2", tag="old0"), sb.tile([P, T], F32, name="faded3", tag="old1")]
@@ -196,23 +203,25 @@ def tile_attend_bsoftlives_b_v_kernel(tc, query, query2, keys_words, keys_scales
             engine.tensor_tensor(acc, acc, windows[k][:, t0:t1], ALU.add)
             nc.sync.dma_start(out=out[P * k : P * (k + 1), t0:t1], in_=acc)
 
-        def scatter(k):
-            nc.scalar.activation(windows[k][:].indirect(offsets[:]), gvs[k], ACT.Copy)
+        def scatter(k, values, i0, i1):
+            nc.scalar.activation(windows[k][:].indirect(offsets[:, i0 // 16 : i1 // 16]), values, ACT.Copy)
 
-        nc.scalar.copy(gv0[:], gv_first[:])
-        fade_half(0, 0)
-        fade_half(0, 1)
-        nc.vector.tensor_copy(gv12[:], gv_pair[:])
-        nc.vector.tensor_copy(gv3[:], gv_last[:])
-        for k in range(4):
-            scatter(k)
+        nc.scalar.copy(head[:], gv_head[:])
+        nc.gpsimd.tensor_tensor(faded[0][:], olds[0][:], fade_sb[:], ALU.mult)
+        fade_half(1, 0)
+        nc.vector.tensor_copy(mid[:], gv_mid[:])
+        nc.vector.tensor_copy(tail[:], gv_tail[:])
+        scatter(0, head[:], 0, P)
+        scatter(0, mid[:, 0:P], P, I)
+        scatter(1, mid[:, P : P + I], 0, I)
+        scatter(2, tail[:, 0:I], 0, I)
+        scatter(3, tail[:, I : 2 * I], 0, I)
         finish(0, 0, T, nc.gpsimd)
-        for k in (1, 2):
+        fade_half(1, 1)
+        for k in (2, 3):
             fade_half(k, 0)
             fade_half(k, 1)
-        fade_half(3, 0)
         finish(1, 0, T, nc.vector)
         finish(2, 0, T, nc.vector)
-        fade_half(3, 1)
         for t0, t1 in ((0, 512), (512, 768), (768, T)):
             finish(3, t0, t1, nc.vector)

from contextlib import ExitStack

import concourse.mybir as mybir
from concourse.masks import make_identity

D, E, T, I, Q = 512, 512, 1024, 256, 512
FLOPS = 2 * (2 * D * Q * I + Q * E * I)
BYTES = 4 * (2 * D * Q + Q * E + 2 * E * T + 2 * T + I + 2 * Q) + 128 * 2 * T + 16 * T + 128 * 16 * 2

F32 = mybir.dt.float32
BF16 = mybir.dt.bfloat16
I32 = mybir.dt.int32
U32 = mybir.dt.uint32
U16 = mybir.dt.uint16
U8 = mybir.dt.uint8
FP8X4 = mybir.dt.float8_e4m3fn_x4
FP4X4 = mybir.dt.float4_e2m1fn_x4
ACT = mybir.ActivationFunctionType
ALU = mybir.AluOpType
AX = mybir.AxisListType

P = 128
PACK = 4
HALF = 256


def tile_attend_bsoftlives_b_v_kernel(tc, query, query2, keys_words, keys_scales, age, grace, size, qs, grows, old, fade, offs, out):
    nc = tc.nc
    with ExitStack() as ctx:
        sb = ctx.enter_context(tc.tile_pool(name="sb", bufs=1))
        ps = ctx.enter_context(tc.psum_pool(name="ps", bufs=1))

        offsets = sb.tile([P, I // 16], U16, name="offsets")
        key_words = sb.tile([P, T], U16, name="key_words")
        key_bytes = sb.tile([P, T], U8, name="key_bytes")
        raw = {}
        for nm in ("query", "query2", "grows"):
            for h in range(2):
                raw[nm, h] = sb.tile([P, PACK, HALF], F32, name="raw_%s%d" % (nm, h), tag="raw_%s%d" % (nm, h))
        fade_col = sb.tile([P, 2, 8], F32, name="fade_col")
        size_col = sb.tile([P, 2], F32, name="size_col")
        grace_t = sb.tile([P, PACK], F32, name="grace_t")
        qs_t = sb.tile([P, PACK], F32, name="qs_t")
        olds = [sb.tile([P, T], F32, name="old%d" % k, tag="old%d" % k) for k in range(4)]
        windows = [sb.tile([P, T], F32, name="window%d" % k) for k in range(4)]
        ident = sb.tile([P, P], F32, name="ident")

        def load_half(src, nm, h):
            nc.sync.dma_start(out=raw[nm, h][:], in_=src.rearrange("(p j) c -> p j c", j=PACK)[:, :, HALF * h : HALF * (h + 1)])

        age_col = sb.tile([P, 2, 8], F32, name="age_col")
        age_g = sb.tile([P, I], F32, name="age_g")
        nc.gpsimd.memset(key_bytes[:].bitcast(I32), 0)
        nc.sync.dma_start(offsets[:], offs)
        nc.sync.dma_start(out=age_col[:, :, 0:4], in_=age[0:1, :].rearrange("o (h p j) -> p (o h) j", h=2, j=4))
        nc.sync.dma_start(out=key_words[:].bitcast(I32), in_=keys_words[0].bitcast(I32))
        load_half(query, "query", 0)
        for g in range(4):
            nc.sync.dma_start(out=key_bytes[32 * g : 32 * g + 4, :].bitcast(I32), in_=keys_scales[0, 4 * g : 4 * g + 4, :].bitcast(I32))
        load_half(query, "query", 1)
        load_half(query2, "query2", 0)
        load_half(query2, "query2", 1)
        nc.sync.dma_start(out=grace_t[:], in_=grace.rearrange("(p r) o -> p (r o)", r=PACK))
        nc.sync.dma_start(out=size_col[:], in_=size.rearrange("o (p j) -> p (o j)", j=2))
        nc.sync.dma_start(out=qs_t[:], in_=qs.rearrange("(p r) o -> p (r o)", r=PACK))
        nc.sync.dma_start(out=fade_col[:, :, 0:4], in_=fade.rearrange("o (h p j) -> p (o h) j", h=2, j=4))
        load_half(grows, "grows", 0)
        load_half(grows, "grows", 1)
        for k in range(4):
            nc.sync.dma_start(out=olds[k][:], in_=old[P * k : P * (k + 1), :])

        make_identity(nc, ident[:])

        def spread(bank, col, first, n):
            for j in range(n):
                nc.tensor.transpose(bank.rearrange("p (n j) -> p j n", j=n)[:, j, :], col[:, first + j : first + j + 1].to_broadcast([P, P]), ident[:])

        kg_words = sb.tile([P, I], U16, name="kg_words", align_bytes=64)
        kg_bytes = sb.tile([P, I], U8, name="kg_bytes", align_bytes=64)
        nc.vector.tensor_copy(kg_words[:], key_words[:].indirect(offsets[:]))
        nc.vector.tensor_copy(kg_bytes[:], key_bytes[:].indirect(offsets[:]))

        codes = {}
        scales = {}
        for nm in ("query", "query2", "grows"):
            codes[nm] = sb.tile([P, 512], U32, name="codes_" + nm, align_bytes=64)
            scales[nm] = sb.tile([P, 512], U8, name="scales_" + nm, align_bytes=64)

        dealt = {nm: sb.tile([P, PACK, P, PACK], BF16, name="dealt_" + nm, align_bytes=64) for nm in ("query", "query2")}

        def round_query(nm, s0, s1, copy):
            h = s0 // 64
            src = raw[nm, h][:, :, PACK * (s0 - 64 * h) : PACK * (s1 - 64 * h)]
            for b in range(2):
                copy(dealt[nm][:, 2 * b : 2 * b + 2, s0:s1, :].rearrange("p r s j -> p s j r"), src.rearrange("p j (s r) -> p s j r", r=PACK)[:, :, :, 2 * b : 2 * b + 2])

        def quantise_query(nm):
            for b in range(2):
                cols = slice(HALF * b, HALF * (b + 1))
                nc.vector.quantize_mx(out=codes[nm][:, cols].bitcast(FP8X4), scales=scales[nm][:, cols], in_=dealt[nm][:, 2 * b : 2 * b + 2, :, :].rearrange("p r s j -> p (r s j)"))

        def scores(nm, tag):
            banks = [ps.tile([P, 2, I], F32, name="%s_ps%d" % (nm, b), tag="%s%d" % (tag, b)) for b in range(2)]
            for r in range(PACK):
                cols = slice(P * r, P * (r + 1))
                nc.tensor.matmul_mx(out=banks[r // 2][:, r % 2, :], lhsT=codes[nm][:, cols].bitcast(FP8X4), lhsT_scale=scales[nm][:, cols],
                                    rhs=kg_words[:].bitcast(FP4X4), rhs_scale=kg_bytes[:], start=True, stop=True)
            return banks

        round_query("query", 0, 64, nc.scalar.copy)
        age_win = sb.tile([P, T], F32, name="age_win", tag="raw_query0")
        for h in range(2):
            bank = ps.tile([P, 512], F32, name="age_ps%d" % h, tag="B%d" % h)
            spread(bank[:], age_col[:, h, :], 0, 4)
            nc.scalar.activation(age_win[:, 512 * h : 512 * (h + 1)], bank[:], ACT.Copy)
        round_query("query", 64, 128, nc.vector.tensor_copy)
        quantise_query("query")
        a_ps = scores("query", "A")

        round_query("query2", 0, 64, nc.scalar.copy)
        neg_max = sb.tile([P, PACK], F32, name="neg_max")
        expo = sb.tile([P, PACK, I], F32, name="expo")
        for b in range(2):
            nc.vector.tensor_reduce(out=neg_max[:, 2 * b : 2 * b + 2], in_=a_ps[b][:], axis=AX.X, op=ALU.max, negate=True)
        for r in range(PACK):
            nc.scalar.activation(expo[:, r, :], a_ps[r // 2][:, r % 2, :], ACT.Exp, bias=neg_max[:, r : r + 1])
        nc.vector.tensor_copy(age_g[:], age_win[:].indirect(offsets[:]))
        round_query("query2", 64, 128, nc.vector.tensor_copy)
        quantise_query("query2")
        b_ps = scores("query2", "B")


        size_ps = ps.tile([P, I], F32, name="size_ps")
        spread(size_ps[:], size_col, 0, 2)
        arg = sb.tile([P, PACK, I], F32, name="arg", tag="arg", align_bytes=64)
        life = sb.tile([P, PACK, I], F32, name="life")
        for r in range(PACK):
            nc.vector.scalar_tensor_tensor(out=arg[:, r, :], in0=b_ps[r // 2][:, r % 2, :], scalar=grace_t[:, r : r + 1], in1=age_g[:], op0=ALU.add, op1=ALU.subtract)
        for r in range(PACK):
            nc.scalar.activation(life[:, r, :], arg[:, r, :], ACT.Sigmoid, scale=3.0)

        fade_ps = [ps.tile([P, 512], F32, name="fade_ps%d" % h, tag="B%d" % h) for h in range(2)]
        for h in range(2):
            spread(fade_ps[h][:], fade_col[:, h, :], 0, 4)

        prob = sb.tile([P, PACK, I], F32, name="prob")
        wq_rows = sb.tile([P, PACK, I], BF16, name="wq_rows")
        factors = []
        for b in range(2):
            total = sb.tile([P, 2], F32, name="total%d" % b)
            inv = sb.tile([P, 2], F32, name="inv%d" % b)
            factor = sb.tile([P, 2], F32, name="factor%d" % b)
            for r in range(2 * b, 2 * b + 2):
                nc.vector.scalar_tensor_tensor(out=prob[:, r, :], in0=expo[:, r, :], scalar=1.0, in1=life[:, r, :], op0=ALU.mult, op1=ALU.mult, accum_out=total[:, r % 2 : r % 2 + 1])
            nc.vector.reciprocal(inv[:], total[:])
            nc.vector.tensor_tensor(factor[:], inv[:], qs_t[:, 2 * b : 2 * b + 2], ALU.mult)
            factors.append(factor)
        for r in range(PACK):
            nc.vector.scalar_tensor_tensor(out=wq_rows[:, r, :], in0=prob[:, r, :], scalar=factors[r // 2][:, r % 2 : r % 2 + 1], in1=size_ps[:], op0=ALU.mult, op1=ALU.mult)
        wq_packed = sb.tile([P, I, PACK], BF16, name="wq_packed", tag="wq_packed", align_bytes=64)
        wq_codes = sb.tile([P, I], U32, name="wq_codes", align_bytes=64)
        wq_scales = sb.tile([P, I], U8, name="wq_scales", align_bytes=64)
        for h in range(2):
            cols = slice(P * h, P * (h + 1))
            nc.vector.tensor_copy(wq_packed[:, cols, :].rearrange("p (c i) r -> p c r i", i=4), wq_rows[:, :, cols].rearrange("p r (c i) -> p c r i", i=4))
        for h in range(2):
            cols = slice(P * h, P * (h + 1))
            nc.vector.quantize_mx(out=wq_codes[:, cols].bitcast(FP8X4), scales=wq_scales[:, cols], in_=wq_packed[:, cols, :].rearrange("p i r -> p (i r)"))

        grows_packed = sb.tile([P, 2, HALF, PACK], BF16, name="grows_packed", tag="arg", align_bytes=64)
        for h in range(2):
            packed = grows_packed[:, h, :, :]
            nc.scalar.copy(packed.rearrange("p (c i) j -> p c j i", i=4), raw["grows", h][:].rearrange("p j (c i) -> p c j i", i=4))
            cols = slice(HALF * h, HALF * (h + 1))
            nc.vector.quantize_mx(out=codes["grows"][:, cols].bitcast(FP8X4), scales=scales["grows"][:, cols], in_=packed.rearrange("p c j -> p (c j)"))

        for k in range(4):
            nc.vector.memset(windows[k][:], 0.0)
        fade_sb = sb.tile([P, T], F32, name="fade_sb")
        for h in range(2):
            nc.scalar.copy(fade_sb[:, 512 * h : 512 * (h + 1)], fade_ps[h][:])

        gv_head = ps.tile([P, P], F32, name="gv_head", tag="A0")
        gv_mid = ps.tile([P, P + I], F32, name="gv_mid", tag="A1")
        gv_tail = ps.tile([P, 2 * I], F32, name="gv_tail")
        for dst, k, i0, i1 in ((gv_head[:], 0, 0, P), (gv_mid[:, 0:P], 0, P, I), (gv_mid[:, P : P + I], 1, 0, I), (gv_tail[:, 0:I], 2, 0, I), (gv_tail[:, I : 2 * I], 3, 0, I)):
            cols = slice(P * k, P * (k + 1))
            nc.tensor.matmul_mx(out=dst, lhsT=codes["grows"][:, cols].bitcast(FP8X4), lhsT_scale=scales["grows"][:, cols],
                                rhs=wq_codes[:, i0:i1].bitcast(FP8X4), rhs_scale=wq_scales[:, i0:i1], start=True, stop=True)
        head = sb.tile([P, P], F32, name="head")
        mid = sb.tile([P, P + I], F32, name="mid")
        tail = sb.tile([P, 2 * I], F32, name="tail")

        faded = [sb.tile([P, T], F32, name="faded0", tag="wq_packed", align_bytes=64), sb.tile([P, T], F32, name="faded1", tag="arg", align_bytes=64),
                 sb.tile([P, T], F32, name="faded2", tag="old0"), sb.tile([P, T], F32, name="faded3", tag="old1")]

        def fade_half(k, h):
            cols = slice(512 * h, 512 * (h + 1))
            nc.vector.tensor_tensor(faded[k][:, cols], olds[k][:, cols], fade_ps[h][:], ALU.mult)

        def finish(k, t0, t1, engine):
            acc = faded[k][:, t0:t1]
            engine.tensor_tensor(acc, acc, windows[k][:, t0:t1], ALU.add)
            nc.sync.dma_start(out=out[P * k : P * (k + 1), t0:t1], in_=acc)

        def scatter(k, values, i0, i1):
            nc.scalar.activation(windows[k][:].indirect(offsets[:, i0 // 16 : i1 // 16]), values, ACT.Copy)

        nc.scalar.copy(head[:], gv_head[:])
        nc.gpsimd.tensor_tensor(faded[0][:], olds[0][:], fade_sb[:], ALU.mult)
        fade_half(1, 0)
        nc.vector.tensor_copy(mid[:], gv_mid[:])
        nc.vector.tensor_copy(tail[:], gv_tail[:])
        scatter(0, head[:], 0, P)
        scatter(0, mid[:, 0:P], P, I)
        scatter(1, mid[:, P : P + I], 0, I)
        scatter(2, tail[:, 0:I], 0, I)
        scatter(3, tail[:, I : 2 * I], 0, I)
        finish(0, 0, T, nc.gpsimd)
        fade_half(1, 1)
        for k in (2, 3):
            fade_half(k, 0)
            fade_half(k, 1)
        finish(1, 0, T, nc.vector)
        finish(2, 0, T, nc.vector)
        for t0, t1 in ((0, 512), (512, 768), (768, T)):
            finish(3, t0, t1, nc.vector)
